import numpy as np
import ml_dtypes


def mxq(x, axis, fmt="e4m3"):
    dtype, down = {"e4m3": (ml_dtypes.float8_e4m3fn, 7), "e5m2": (ml_dtypes.float8_e5m2, 14)}[fmt]
    v = np.moveaxis(np.asarray(x, np.float32).astype(ml_dtypes.bfloat16).astype(np.float64), axis, -1)
    blocks = v.reshape(v.shape[:-1] + (-1, 32))
    amax = np.abs(blocks).max(-1, keepdims=True)
    byte = np.maximum(np.where(amax > 0, np.frexp(amax)[1] - 1 + 127, 0) - down, 1)
    scale = np.exp2(byte - 127.0)
    codes = (blocks / scale).astype(np.float32).astype(dtype).astype(np.float64)
    return np.moveaxis((codes * scale).reshape(v.shape), -1, axis)


WIDE = False


def mx_kscale(k):
    if not WIDE:
        return np.ones(k)
    levels = np.array([30, -30])
    if k % 512:
        return np.exp2(np.random.permutation(np.resize(levels, k // 32))).repeat(32)
    a = np.empty((k // 512, 16))
    for p in range(k // 512):
        a[p, :8] = np.random.permutation(np.resize(levels, 8))
        for g in range(8):
            far = levels[np.abs(levels - a[p, g]) >= 10]
            a[p, g + 8] = far[np.random.randint(len(far))]
    return np.exp2(a.ravel()).repeat(32)


def f64(x):
    return np.asarray(x).astype(np.float64)


def striped(idx):
    return np.tile(np.asarray(idx).reshape(-1, 16).T, (8, 1)).astype(np.uint16)


def unstriped(offs):
    return offs[:16].T.reshape(-1).astype(np.int64)


E2M1 = np.array([0.0, 0.5, 1.0, 1.5, 2.0, 3.0, 4.0, 6.0, -0.0, -0.5, -1.0, -1.5, -2.0, -3.0, -4.0, -6.0])


def pack_weight(w, fmt):
    k, n = w.shape
    w = f64(np.asarray(w, np.float32).astype(ml_dtypes.bfloat16)).reshape(k // 32, 32, n)
    amax = np.abs(w).max(1)
    if fmt in ("e4m3", "e5m2"):
        byte = np.frexp(amax)[1] - 1 + 127 - (7 if fmt == "e4m3" else 14)
    else:
        mant, ex = np.frexp(amax / 6.0)
        byte = np.where(mant > 0.5, ex, ex - 1) + 127
    byte = np.clip(np.where(amax > 0, byte, 1), 1, 254)
    scaled = (w * np.exp2(127.0 - byte)[:, None, :]).reshape(k, n).astype(np.float32)
    by_word = np.ascontiguousarray(scaled.reshape(k // 512, 128, 4, n).transpose(0, 1, 3, 2))
    if fmt in ("e4m3", "e5m2"):
        words = by_word.astype(ml_dtypes.float8_e4m3fn if fmt == "e4m3" else ml_dtypes.float8_e5m2).view(np.uint8)
    else:
        c = by_word.astype(ml_dtypes.float4_e2m1fn).view(np.uint8) & 0xF
        words = (c[..., 0::2] | (c[..., 1::2] << 4)).reshape(k // 512, 128, 2 * n)
    return np.ascontiguousarray(words), np.ascontiguousarray(byte.astype(np.uint8).reshape(k // 512, 16, n))


def unpack_weight(words, scales, fmt):
    g, _, n = scales.shape
    words = np.ascontiguousarray(words).reshape(g, 128, n, -1)
    if fmt in ("e4m3", "e5m2"):
        vals = words.view(ml_dtypes.float8_e4m3fn if fmt == "e4m3" else ml_dtypes.float8_e5m2).astype(np.float64)
    else:
        nib = np.empty((g, 128, n, 4), np.uint8)
        nib[..., 0::2] = words & 0xF
        nib[..., 1::2] = words >> 4
        vals = E2M1[nib]
    vals = vals * np.repeat(np.exp2(scales.astype(np.float64) - 127.0), 8, axis=1)[..., None]
    return vals.transpose(0, 1, 3, 2).reshape(g * 512, n)


def sigmoid(v):
    return 1.0 / (1.0 + np.exp(-v))


K, T, J, R, C, O, N, E = 512, 2048, 256, 512, 512, 256, 256, 1024


def setup_inputs():
    n = np.random.standard_normal
    idx = np.random.permutation(T)[:J]
    idx2 = np.random.permutation(T)[:J]
    idx3 = np.random.permutation(C)[:J]
    idx4 = np.random.permutation(C)[:J]
    idx5 = np.random.permutation(C)[:O]
    idx6 = np.random.permutation(E)[:O]
    fk = mx_kscale(K)
    fr = mx_kscale(R)
    xtp = pack_weight(n((K, T)) / fk[:, None], "e5m2")
    wp = pack_weight(n((K, R)) * 1 / np.sqrt(K) * fk[:, None] * fr, "e2m1")
    wbp = pack_weight(n((R, N)) * 1 / np.sqrt(R) / fr[:, None], "e2m1")
    return {
        "xt_words": xtp[0],
        "xt_scales": xtp[1],
        "w_words": wp[0],
        "w_scales": wp[1],
        "wb_words": wbp[0],
        "wb_scales": wbp[1],
        "tz": (n((N, E))).astype(np.float32),
        "so": (np.random.uniform(0.6, 1.6, (N, 1))).astype(np.float32),
        "bo": (np.random.uniform(-1.0, 1.0, (N, 1))).astype(np.float32),
        "offs": striped(idx),
        "offs2": striped(idx2),
        "offs3": striped(idx3),
        "offs4": striped(idx4),
        "offs5": striped(idx5),
        "offs6": striped(idx6),
    }


def reference(xt_words, xt_scales, w_words, w_scales, wb_words, wb_scales, tz, so, bo, offs, offs2, offs3, offs4, offs5, offs6):
    idx = unstriped(offs)
    idx2 = unstriped(offs2)
    idx3 = unstriped(offs3)
    idx4 = unstriped(offs4)
    idx5 = unstriped(offs5)
    idx6 = unstriped(offs6)
    xtu = unpack_weight(xt_words, xt_scales, "e5m2")
    wu = unpack_weight(w_words, w_scales, "e2m1")
    wbu = unpack_weight(wb_words, wb_scales, "e2m1")
    xtidxg = xtu[:, idx]
    a = wu.T @ xtidxg
    xtidx2g = xtu[:, idx2]
    b = wu.T @ xtidx2g
    pw = np.zeros((R, C))
    pw[:, idx3] = a
    pv = np.zeros((R, C))
    pv[:, idx4] = b
    pg = pw + pv
    hid = pg[:, idx5]
    hidq = mxq(hid, 0, "e4m3")
    p = wbu.T @ hidq
    y = p * sigmoid(f64(tz)[:, idx6] * f64(so) + f64(bo))
    return y

@@ -1,0 +1,178 @@
+from contextlib import ExitStack
+
+import concourse.mybir as mybir
+
+K, T, J, R, C, O, N, E = 512, 2048, 256, 512, 512, 256, 256, 1024
+FLOPS = 2 * K * R * 2 * J + 2 * R * N * O
+
+F32 = mybir.dt.float32
+BF16 = mybir.dt.bfloat16
+I32 = mybir.dt.int32
+U32 = mybir.dt.uint32
+U16 = mybir.dt.uint16
+U8 = mybir.dt.uint8
+E5M2 = mybir.dt.float8_e5m2_x4
+E4M3 = mybir.dt.float8_e4m3fn_x4
+E2M1 = mybir.dt.float4_e2m1fn_x4
+ACT = mybir.ActivationFunctionType
+ADD = mybir.AluOpType.add
+MULT = mybir.AluOpType.mult
+
+P = 128
+PACK = 4
+RING = 3
+
+
+def load_scale_rows(nc, plane, scales):
+    for q in range(4):
+        nc.sync.dma_start(out=plane[32 * q : 32 * q + 4, :].bitcast(I32), in_=scales[0, 4 * q : 4 * q + 4, :].bitcast(I32))
+
+
+def tile_list_tied_shared_one_finalgate_kernel(
+    tc, xt_words, xt_scales, w_words, w_scales, wb_words, wb_scales, tz, so, bo, offs, offs2, offs3, offs4, offs5, offs6, out
+):
+    nc = tc.nc
+    with ExitStack() as ctx:
+        lists = ctx.enter_context(tc.tile_pool(name="lists", bufs=1))
+        keep = ctx.enter_context(tc.tile_pool(name="keep", bufs=1))
+        psum = ctx.enter_context(tc.psum_pool(name="psum", bufs=1))
+
+        def load_list(src, name):
+            tile = lists.tile([P, J // 16], U16, name=name)
+            nc.sync.dma_start(tile[:], src)
+            return tile
+
+        ws_raw = keep.tile([P, R], U8, name="ws_raw", align_bytes=64)
+        nc.vector.memset(ws_raw[:].bitcast(I32), 0)
+        xs = keep.tile([P, T], U8, name="xs", tag="second_table", align_bytes=64)
+        nc.vector.memset(xs[:].bitcast(I32), 0)
+
+        ww_raw = keep.tile([P, R], U16, name="ww_raw", align_bytes=64)
+        nc.scalar.dma_start(out=ww_raw[:].bitcast(I32), in_=w_words[0].bitcast(I32))
+        wbw = keep.tile([P, N], U16, name="wbw", align_bytes=64)
+        nc.scalar.dma_start(out=wbw[:].bitcast(I32), in_=wb_words[0].bitcast(I32))
+        slope = keep.tile([P, 2], F32, name="slope")
+        with nc.allow_non_contiguous_dma(reason="one value a partition and half"):
+            nc.scalar.dma_start(out=slope[:], in_=so.rearrange("(h p) o -> p (h o)", p=P))
+        xw = keep.tile([P, T], U32, name="xw", tag="first_table", align_bytes=64)
+        nc.scalar.dma_start(out=xw[:].bitcast(I32), in_=xt_words[0].rearrange("p n t -> p (n t)").bitcast(I32))
+
+        tok_a = load_list(offs, "tok_a")
+        load_scale_rows(nc, ws_raw, w_scales)
+        load_scale_rows(nc, xs, xt_scales)
+        tok_b = load_list(offs2, "tok_b")
+        col_a = load_list(offs3, "col_a")
+        col_b = load_list(offs4, "col_b")
+        reads = load_list(offs5, "reads")
+        gates = load_list(offs6, "gates")
+        shift = keep.tile([P, 2], F32, name="shift")
+        with nc.allow_non_contiguous_dma(reason="one value a partition and half"):
+            nc.sync.dma_start(out=shift[:], in_=bo.rearrange("(h p) o -> p (h o)", p=P))
+
+        board_a = [keep.tile([P, C], F32, name=f"board_a{i}") for i in range(RING)]
+        board_b = [keep.tile([P, C], F32, name=f"board_b{i}") for i in range(RING)]
+        for i in range(RING):
+            nc.vector.memset(board_a[i][:], 0.0)
+            nc.vector.memset(board_b[i][:], 0.0)
+
+        ww = keep.tile([P, R], U16, name="ww", align_bytes=64)
+        nc.vector.tensor_copy(
+            out=ww[:].rearrange("p (t c i) -> p c t i", t=PACK, i=8),
+            in_=ww_raw[:].rearrange("p (c i t) -> p c t i", t=PACK, i=8),
+        )
+        ws = keep.tile([P, R], U8, name="ws", align_bytes=64)
+        nc.vector.tensor_copy(
+            out=ws[:].rearrange("p (t c i) -> p c t i", t=PACK, i=16),
+            in_=ws_raw[:].rearrange("p (c i t) -> p c t i", t=PACK, i=16),
+        )
+
+        banks = []
+        for name, tok in (("a", tok_a), ("b", tok_b)):
+            gw = keep.tile([P, J], U32, name=f"gw_{name}", align_bytes=64)
+            nc.vector.tensor_copy(out=gw[:], in_=xw[:].indirect(tok[:]))
+            gs = keep.tile([P, J], U8, name=f"gs_{name}", align_bytes=64)
+            nc.vector.tensor_copy(out=gs[:], in_=xs[:].indirect(tok[:]))
+            for t in range(PACK):
+                cols = slice(P * t, P * (t + 1))
+                acc = psum.tile([P, J], F32, name=f"acc_{name}{t}")
+                nc.tensor.matmul_mx(
+                    out=acc[:], lhsT=ww[:, cols].bitcast(E2M1), lhsT_scale=ws[:, cols],
+                    rhs=gw[:].bitcast(E5M2), rhs_scale=gs[:], start=True, stop=True,
+                )
+                banks.append(acc)
+
+        load_scale_rows(nc, ws_raw[:, 0:N], wb_scales)
+        table = []
+        for h, tag in enumerate(("first_table", "second_table")):
+            rows = keep.tile([P, E], F32, name=f"tz{h}", tag=tag, align_bytes=64)
+            nc.sync.dma_start(out=rows[:], in_=tz[P * h : P * (h + 1), :])
+            table.append(rows)
+
+        hid = keep.tile([P, PACK, O], F32, name="hid")
+        sum_a = [keep.tile([P, J], F32, name=f"sum_a{t}") for t in range(PACK)]
+        sum_b = [keep.tile([P, J], F32, name=f"sum_b{t}") for t in range(PACK)]
+        pg = [keep.tile([P, C], F32, name=f"pg{t}", tag=f"pg{t}") for t in range(PACK)]
+
+        def fetch_a(t):
+            nc.scalar.activation(out=sum_a[t][:], in_=banks[t][:], func=ACT.Copy)
+
+        def place(t):
+            if t + 1 < PACK:
+                fetch_a(t + 1)
+            nc.scalar.activation(out=board_a[t % RING][:].indirect(col_a[:]), in_=sum_a[t][:], func=ACT.Copy)
+            nc.vector.tensor_copy(out=board_b[t % RING][:].indirect(col_b[:]), in_=sum_b[t][:])
+            if t + 1 < PACK:
+                nc.scalar.activation(out=sum_b[t + 1][:], in_=banks[PACK + t + 1][:], func=ACT.Copy)
+
+        def join(t):
+            nc.vector.tensor_tensor(out=pg[t][:], in0=board_a[t % RING][:], in1=board_b[t % RING][:], op=ADD)
+
+        def read(t):
+            nc.scalar.activation(out=hid[:, t, :], in_=pg[t][:].indirect(reads[:]), func=ACT.Copy)
+
+        fetch_a(0)
+        nc.vector.tensor_copy(out=sum_b[0][:], in_=banks[PACK][:])
+        for step in range(PACK + 1):
+            if step < PACK:
+                place(step)
+            if step >= 1:
+                join(step - 1)
+            if step >= 2:
+                read(step - 2)
+        last = PACK - 1
+        half = O // 2
+        nc.vector.tensor_copy(out=hid[:, last, 0:half], in_=pg[last][:].indirect(reads[:, 0 : half // 16]))
+        nc.scalar.activation(out=hid[:, last, half:O], in_=pg[last][:].indirect(reads[:, half // 16 : O // 16]), func=ACT.Copy)
+
+        gate = keep.tile([P, 2, O], F32, name="gate", tag=f"pg{last}")
+        for h in range(2):
+            nc.scalar.activation(
+                out=gate[:, h, :], in_=table[h][:].indirect(gates[:]), func=ACT.Sigmoid,
+                scale=slope[:, h : h + 1], bias=shift[:, h : h + 1],
+            )
+
+        hid16 = [keep.tile([P, half * PACK], BF16, name=f"hid16_{u}", align_bytes=64) for u in range(2)]
+        for u in range(2):
+            nc.vector.tensor_copy(
+                out=hid16[u][:].rearrange("p (c i t) -> p c t i", t=PACK, i=4),
+                in_=hid[:, :, half * u : half * (u + 1)].rearrange("p t (c i) -> p c t i", i=4),
+            )
+
+        prod = []
+        for u in range(2):
+            hq = keep.tile([P, half], U32, name=f"hq{u}", align_bytes=64)
+            hs = keep.tile([P, half], U8, name=f"hs{u}", align_bytes=64)
+            nc.vector.quantize_mx(out=hq[:].bitcast(E4M3), scales=hs[:], in_=hid16[u][:])
+            acc = psum.tile([P, 2, half], F32, name=f"prod{u}", tag=f"acc_a{u}")
+            for h in range(2):
+                cols = slice(P * h, P * (h + 1))
+                nc.tensor.matmul_mx(
+                    out=acc[:, h, :], lhsT=wbw[:, cols].bitcast(E2M1), lhsT_scale=ws_raw[:, cols],
+                    rhs=hq[:].bitcast(E4M3), rhs_scale=hs[:], start=True, stop=True,
+                )
+            prod.append(acc)
+        for u in range(2):
+            reads_u = slice(half * u, half * (u + 1))
+            res = keep.tile([P, 2, half], F32, name=f"res{u}")
+            nc.vector.tensor_tensor(out=res[:], in0=prod[u][:], in1=gate[:, :, reads_u], op=MULT)
+            (nc.sync if u == 0 else nc.scalar).dma_start(out=out[:, reads_u].rearrange("(h p) o -> p h o", p=P), in_=res[:])

@@ -57,6 +57,10 @@ def tile_list_tied_shared_one_finalgate_kernel(
         xw = keep.tile([P, T], U32, name="xw", tag="first_table", align_bytes=64)
         nc.scalar.dma_start(out=xw[:].bitcast(I32), in_=xt_words[0].rearrange("p n t -> p (n t)").bitcast(I32))
 
+        warm = keep.tile([P, 16], F32, name="warm")
+        nc.gpsimd.memset(warm[:, 0:8], 0.0)
+        nc.scalar.activation(out=warm[:, 8:9], in_=warm[:, 0:1], func=ACT.Sigmoid)
+
         tok_a = load_list(offs, "tok_a")
         load_scale_rows(nc, ws_raw, w_scales)
         load_scale_rows(nc, xs, xt_scales)

@@ -20,12 +20,14 @@ MULT = mybir.AluOpType.mult
 
 P = 128
 PACK = 4
-RING = 3
+VECTOR_FETCHES = 4
+RING_A = 3
+RING_B = 2
 
 
-def load_scale_rows(nc, plane, scales):
-    for q in range(4):
-        nc.sync.dma_start(out=plane[32 * q : 32 * q + 4, :].bitcast(I32), in_=scales[0, 4 * q : 4 * q + 4, :].bitcast(I32))
+def load_scale_rows(queue, plane, scales, quadrants=range(4)):
+    for q in quadrants:
+        queue.dma_start(out=plane[32 * q : 32 * q + 4, :].bitcast(I32), in_=scales[0, 4 * q : 4 * q + 4, :].bitcast(I32))
 
 
 def tile_list_tied_shared_one_finalgate_kernel(
@@ -47,13 +49,9 @@ def tile_list_tied_shared_one_finalgate_kernel(
         xs = keep.tile([P, T], U8, name="xs", tag="second_table", align_bytes=64)
         nc.vector.memset(xs[:].bitcast(I32), 0)
 
-        ww_raw = keep.tile([P, R], U16, name="ww_raw", align_bytes=64)
+        ww_raw = keep.tile([P, R], U16, name="ww_raw", tag="weight_words", align_bytes=64)
         nc.scalar.dma_start(out=ww_raw[:].bitcast(I32), in_=w_words[0].bitcast(I32))
-        wbw = keep.tile([P, N], U16, name="wbw", align_bytes=64)
-        nc.scalar.dma_start(out=wbw[:].bitcast(I32), in_=wb_words[0].bitcast(I32))
-        slope = keep.tile([P, 2], F32, name="slope")
-        with nc.allow_non_contiguous_dma(reason="one value a partition and half"):
-            nc.scalar.dma_start(out=slope[:], in_=so.rearrange("(h p) o -> p (h o)", p=P))
+        load_scale_rows(nc.scalar, ws_raw, w_scales, range(0, 1))
         xw = keep.tile([P, T], U32, name="xw", tag="first_table", align_bytes=64)
         nc.scalar.dma_start(out=xw[:].bitcast(I32), in_=xt_words[0].rearrange("p n t -> p (n t)").bitcast(I32))
 
@@ -62,22 +60,23 @@ def tile_list_tied_shared_one_finalgate_kernel(
         nc.scalar.activation(out=warm[:, 8:9], in_=warm[:, 0:1], func=ACT.Sigmoid)
 
         tok_a = load_list(offs, "tok_a")
-        load_scale_rows(nc, ws_raw, w_scales)
-        load_scale_rows(nc, xs, xt_scales)
+        load_scale_rows(nc.sync, ws_raw, w_scales, range(1, 4))
+        load_scale_rows(nc.sync, xs, xt_scales)
         tok_b = load_list(offs2, "tok_b")
         col_a = load_list(offs3, "col_a")
         col_b = load_list(offs4, "col_b")
         reads = load_list(offs5, "reads")
         gates = load_list(offs6, "gates")
+        slope = keep.tile([P, 2], F32, name="slope")
         shift = keep.tile([P, 2], F32, name="shift")
         with nc.allow_non_contiguous_dma(reason="one value a partition and half"):
+            nc.sync.dma_start(out=slope[:], in_=so.rearrange("(h p) o -> p (h o)", p=P))
             nc.sync.dma_start(out=shift[:], in_=bo.rearrange("(h p) o -> p (h o)", p=P))
 
-        board_a = [keep.tile([P, C], F32, name=f"board_a{i}") for i in range(RING)]
-        board_b = [keep.tile([P, C], F32, name=f"board_b{i}") for i in range(RING)]
-        for i in range(RING):
-            nc.vector.memset(board_a[i][:], 0.0)
-            nc.vector.memset(board_b[i][:], 0.0)
+        board_a = [keep.tile([P, C], F32, name=f"board_a{i}") for i in range(RING_A)]
+        board_b = [keep.tile([P, C], F32, name=f"board_b{i}") for i in range(RING_B)]
+        for board in board_a + board_b:
+            nc.vector.memset(board[:].bitcast(I32), 0)
 
         ww = keep.tile([P, R], U16, name="ww", align_bytes=64)
         nc.vector.tensor_copy(
@@ -105,7 +104,9 @@ def tile_list_tied_shared_one_finalgate_kernel(
                 )
                 banks.append(acc)
 
-        load_scale_rows(nc, ws_raw[:, 0:N], wb_scales)
+        wbw = keep.tile([P, N], U16, name="wbw", tag="weight_words", align_bytes=64)
+        nc.sync.dma_start(out=wbw[:].bitcast(I32), in_=wb_words[0].bitcast(I32))
+        load_scale_rows(nc.sync, ws_raw[:, 0:N], wb_scales)
         table = []
         for h, tag in enumerate(("first_table", "second_table")):
             rows = keep.tile([P, E], F32, name=f"tz{h}", tag=tag, align_bytes=64)
@@ -123,13 +124,15 @@ def tile_list_tied_shared_one_finalgate_kernel(
         def place(t):
             if t + 1 < PACK:
                 fetch_a(t + 1)
-            nc.scalar.activation(out=board_a[t % RING][:].indirect(col_a[:]), in_=sum_a[t][:], func=ACT.Copy)
-            nc.vector.tensor_copy(out=board_b[t % RING][:].indirect(col_b[:]), in_=sum_b[t][:])
-            if t + 1 < PACK:
+            nc.scalar.activation(out=board_a[t % RING_A][:].indirect(col_a[:]), in_=sum_a[t][:], func=ACT.Copy)
+            nc.vector.tensor_copy(out=board_b[t % RING_B][:].indirect(col_b[:]), in_=sum_b[t][:])
+            if t + 1 < VECTOR_FETCHES:
+                nc.vector.tensor_copy(out=sum_b[t + 1][:], in_=banks[PACK + t + 1][:])
+            elif t + 1 < PACK:
                 nc.scalar.activation(out=sum_b[t + 1][:], in_=banks[PACK + t + 1][:], func=ACT.Copy)
 
         def join(t):
-            nc.vector.tensor_tensor(out=pg[t][:], in0=board_a[t % RING][:], in1=board_b[t % RING][:], op=ADD)
+            (nc.gpsimd if t + 1 < PACK else nc.vector).tensor_tensor(out=pg[t][:], in0=board_a[t % RING_A][:], in1=board_b[t % RING_B][:], op=ADD)
 
         def read(t):
             nc.scalar.activation(out=hid[:, t, :], in_=pg[t][:].indirect(reads[:]), func=ACT.Copy)
@@ -139,16 +142,18 @@ def tile_list_tied_shared_one_finalgate_kernel(
         for step in range(PACK + 1):
             if step < PACK:
                 place(step)
-            if step >= 1:
-                join(step - 1)
+                join(step)
             if step >= 2:
                 read(step - 2)
         last = PACK - 1
         half = O // 2
-        nc.vector.tensor_copy(out=hid[:, last, 0:half], in_=pg[last][:].indirect(reads[:, 0 : half // 16]))
-        nc.scalar.activation(out=hid[:, last, half:O], in_=pg[last][:].indirect(reads[:, half // 16 : O // 16]), func=ACT.Copy)
+        for u in range(2):
+            nc.vector.tensor_copy(
+                out=hid[:, last, half * u : half * (u + 1)],
+                in_=pg[last][:].indirect(reads[:, half // 16 * u : half // 16 * (u + 1)]),
+            )
 
-        gate = keep.tile([P, 2, O], F32, name="gate", tag=f"pg{last}")
+        gate = keep.tile([P, 2, O], F32, name="gate", tag=f"pg{last - 1}")
         for h in range(2):
             nc.scalar.activation(
                 out=gate[:, h, :], in_=table[h][:].indirect(gates[:]), func=ACT.Sigmoid,

@@ -20,7 +20,7 @@ MULT = mybir.AluOpType.mult
 
 P = 128
 PACK = 4
-VECTOR_FETCHES = 4
+VECTOR_FETCHES = 3
 RING_A = 3
 RING_B = 2
 

from contextlib import ExitStack

import concourse.mybir as mybir

K, T, J, R, C, O, N, E = 512, 2048, 256, 512, 512, 256, 256, 1024
FLOPS = 2 * K * R * 2 * J + 2 * R * N * O

F32 = mybir.dt.float32
BF16 = mybir.dt.bfloat16
I32 = mybir.dt.int32
U32 = mybir.dt.uint32
U16 = mybir.dt.uint16
U8 = mybir.dt.uint8
E5M2 = mybir.dt.float8_e5m2_x4
E4M3 = mybir.dt.float8_e4m3fn_x4
E2M1 = mybir.dt.float4_e2m1fn_x4
ACT = mybir.ActivationFunctionType
ADD = mybir.AluOpType.add
MULT = mybir.AluOpType.mult

P = 128
PACK = 4
VECTOR_FETCHES = 3
RING_A = 3
RING_B = 2


def load_scale_rows(queue, plane, scales, quadrants=range(4)):
    for q in quadrants:
        queue.dma_start(out=plane[32 * q : 32 * q + 4, :].bitcast(I32), in_=scales[0, 4 * q : 4 * q + 4, :].bitcast(I32))


def tile_list_tied_shared_one_finalgate_kernel(
    tc, xt_words, xt_scales, w_words, w_scales, wb_words, wb_scales, tz, so, bo, offs, offs2, offs3, offs4, offs5, offs6, out
):
    nc = tc.nc
    with ExitStack() as ctx:
        lists = ctx.enter_context(tc.tile_pool(name="lists", bufs=1))
        keep = ctx.enter_context(tc.tile_pool(name="keep", bufs=1))
        psum = ctx.enter_context(tc.psum_pool(name="psum", bufs=1))

        def load_list(src, name):
            tile = lists.tile([P, J // 16], U16, name=name)
            nc.sync.dma_start(tile[:], src)
            return tile

        ws_raw = keep.tile([P, R], U8, name="ws_raw", align_bytes=64)
        nc.vector.memset(ws_raw[:].bitcast(I32), 0)
        xs = keep.tile([P, T], U8, name="xs", tag="second_table", align_bytes=64)
        nc.vector.memset(xs[:].bitcast(I32), 0)

        ww_raw = keep.tile([P, R], U16, name="ww_raw", tag="weight_words", align_bytes=64)
        nc.scalar.dma_start(out=ww_raw[:].bitcast(I32), in_=w_words[0].bitcast(I32))
        load_scale_rows(nc.scalar, ws_raw, w_scales, range(0, 1))
        xw = keep.tile([P, T], U32, name="xw", tag="first_table", align_bytes=64)
        nc.scalar.dma_start(out=xw[:].bitcast(I32), in_=xt_words[0].rearrange("p n t -> p (n t)").bitcast(I32))

        warm = keep.tile([P, 16], F32, name="warm")
        nc.gpsimd.memset(warm[:, 0:8], 0.0)
        nc.scalar.activation(out=warm[:, 8:9], in_=warm[:, 0:1], func=ACT.Sigmoid)

        tok_a = load_list(offs, "tok_a")
        load_scale_rows(nc.sync, ws_raw, w_scales, range(1, 4))
        load_scale_rows(nc.sync, xs, xt_scales)
        tok_b = load_list(offs2, "tok_b")
        col_a = load_list(offs3, "col_a")
        col_b = load_list(offs4, "col_b")
        reads = load_list(offs5, "reads")
        gates = load_list(offs6, "gates")
        slope = keep.tile([P, 2], F32, name="slope")
        shift = keep.tile([P, 2], F32, name="shift")
        with nc.allow_non_contiguous_dma(reason="one value a partition and half"):
            nc.sync.dma_start(out=slope[:], in_=so.rearrange("(h p) o -> p (h o)", p=P))
            nc.sync.dma_start(out=shift[:], in_=bo.rearrange("(h p) o -> p (h o)", p=P))

        board_a = [keep.tile([P, C], F32, name=f"board_a{i}") for i in range(RING_A)]
        board_b = [keep.tile([P, C], F32, name=f"board_b{i}") for i in range(RING_B)]
        for board in board_a + board_b:
            nc.vector.memset(board[:].bitcast(I32), 0)

        ww = keep.tile([P, R], U16, name="ww", align_bytes=64)
        nc.vector.tensor_copy(
            out=ww[:].rearrange("p (t c i) -> p c t i", t=PACK, i=8),
            in_=ww_raw[:].rearrange("p (c i t) -> p c t i", t=PACK, i=8),
        )
        ws = keep.tile([P, R], U8, name="ws", align_bytes=64)
        nc.vector.tensor_copy(
            out=ws[:].rearrange("p (t c i) -> p c t i", t=PACK, i=16),
            in_=ws_raw[:].rearrange("p (c i t) -> p c t i", t=PACK, i=16),
        )

        banks = []
        for name, tok in (("a", tok_a), ("b", tok_b)):
            gw = keep.tile([P, J], U32, name=f"gw_{name}", align_bytes=64)
            nc.vector.tensor_copy(out=gw[:], in_=xw[:].indirect(tok[:]))
            gs = keep.tile([P, J], U8, name=f"gs_{name}", align_bytes=64)
            nc.vector.tensor_copy(out=gs[:], in_=xs[:].indirect(tok[:]))
            for t in range(PACK):
                cols = slice(P * t, P * (t + 1))
                acc = psum.tile([P, J], F32, name=f"acc_{name}{t}")
                nc.tensor.matmul_mx(
                    out=acc[:], lhsT=ww[:, cols].bitcast(E2M1), lhsT_scale=ws[:, cols],
                    rhs=gw[:].bitcast(E5M2), rhs_scale=gs[:], start=True, stop=True,
                )
                banks.append(acc)

        wbw = keep.tile([P, N], U16, name="wbw", tag="weight_words", align_bytes=64)
        nc.sync.dma_start(out=wbw[:].bitcast(I32), in_=wb_words[0].bitcast(I32))
        load_scale_rows(nc.sync, ws_raw[:, 0:N], wb_scales)
        table = []
        for h, tag in enumerate(("first_table", "second_table")):
            rows = keep.tile([P, E], F32, name=f"tz{h}", tag=tag, align_bytes=64)
            nc.sync.dma_start(out=rows[:], in_=tz[P * h : P * (h + 1), :])
            table.append(rows)

        hid = keep.tile([P, PACK, O], F32, name="hid")
        sum_a = [keep.tile([P, J], F32, name=f"sum_a{t}") for t in range(PACK)]
        sum_b = [keep.tile([P, J], F32, name=f"sum_b{t}") for t in range(PACK)]
        pg = [keep.tile([P, C], F32, name=f"pg{t}", tag=f"pg{t}") for t in range(PACK)]

        def fetch_a(t):
            nc.scalar.activation(out=sum_a[t][:], in_=banks[t][:], func=ACT.Copy)

        def place(t):
            if t + 1 < PACK:
                fetch_a(t + 1)
            nc.scalar.activation(out=board_a[t % RING_A][:].indirect(col_a[:]), in_=sum_a[t][:], func=ACT.Copy)
            nc.vector.tensor_copy(out=board_b[t % RING_B][:].indirect(col_b[:]), in_=sum_b[t][:])
            if t + 1 < VECTOR_FETCHES:
                nc.vector.tensor_copy(out=sum_b[t + 1][:], in_=banks[PACK + t + 1][:])
            elif t + 1 < PACK:
                nc.scalar.activation(out=sum_b[t + 1][:], in_=banks[PACK + t + 1][:], func=ACT.Copy)

        def join(t):
            (nc.gpsimd if t + 1 < PACK else nc.vector).tensor_tensor(out=pg[t][:], in0=board_a[t % RING_A][:], in1=board_b[t % RING_B][:], op=ADD)

        def read(t):
            nc.scalar.activation(out=hid[:, t, :], in_=pg[t][:].indirect(reads[:]), func=ACT.Copy)

        fetch_a(0)
        nc.vector.tensor_copy(out=sum_b[0][:], in_=banks[PACK][:])
        for step in range(PACK + 1):
            if step < PACK:
                place(step)
                join(step)
            if step >= 2:
                read(step - 2)
        last = PACK - 1
        half = O // 2
        for u in range(2):
            nc.vector.tensor_copy(
                out=hid[:, last, half * u : half * (u + 1)],
                in_=pg[last][:].indirect(reads[:, half // 16 * u : half // 16 * (u + 1)]),
            )

        gate = keep.tile([P, 2, O], F32, name="gate", tag=f"pg{last - 1}")
        for h in range(2):
            nc.scalar.activation(
                out=gate[:, h, :], in_=table[h][:].indirect(gates[:]), func=ACT.Sigmoid,
                scale=slope[:, h : h + 1], bias=shift[:, h : h + 1],
            )

        hid16 = [keep.tile([P, half * PACK], BF16, name=f"hid16_{u}", align_bytes=64) for u in range(2)]
        for u in range(2):
            nc.vector.tensor_copy(
                out=hid16[u][:].rearrange("p (c i t) -> p c t i", t=PACK, i=4),
                in_=hid[:, :, half * u : half * (u + 1)].rearrange("p t (c i) -> p c t i", i=4),
            )

        prod = []
        for u in range(2):
            hq = keep.tile([P, half], U32, name=f"hq{u}", align_bytes=64)
            hs = keep.tile([P, half], U8, name=f"hs{u}", align_bytes=64)
            nc.vector.quantize_mx(out=hq[:].bitcast(E4M3), scales=hs[:], in_=hid16[u][:])
            acc = psum.tile([P, 2, half], F32, name=f"prod{u}", tag=f"acc_a{u}")
            for h in range(2):
                cols = slice(P * h, P * (h + 1))
                nc.tensor.matmul_mx(
                    out=acc[:, h, :], lhsT=wbw[:, cols].bitcast(E2M1), lhsT_scale=ws_raw[:, cols],
                    rhs=hq[:].bitcast(E4M3), rhs_scale=hs[:], start=True, stop=True,
                )
            prod.append(acc)
        for u in range(2):
            reads_u = slice(half * u, half * (u + 1))
            res = keep.tile([P, 2, half], F32, name=f"res{u}")
            nc.vector.tensor_tensor(out=res[:], in0=prod[u][:], in1=gate[:, :, reads_u], op=MULT)
            (nc.sync if u == 0 else nc.scalar).dma_start(out=out[:, reads_u].rearrange("(h p) o -> p h o", p=P), in_=res[:])
